import numpy as np, ml_dtypes
CORES = [89,94,345,350]
N = 4
import mx_ref
NC, G = 128, 2
C = np.float32(0.00048828125)
BF = ml_dtypes.bfloat16
def cut(t, i, w=512):
    return t[:, w * i:w * i + w]
def tile(rs):
    return np.stack(rs, axis=2).reshape(128, -1).astype(BF)
def layer(w, X):
    out = []
    for i in range(G):
        for t in range(len(X)):
            p = mx_ref.matmul(mx_ref.quantize(cut(w, len(X) * i + t)), X[t])
            z = p if t == 0 else z + p
        out.append(z)
    return out
def gate(U, V):
    return [(np.maximum(s * u, 0) * v) * C for u, v in zip(U, V) for s in (1, -1)]
def setup_inputs(rng):
    def f(*shape):
        return mx_ref.flush((rng.standard_normal(shape, dtype=np.float32) * np.exp2(rng.integers(-2, 3, shape[:-1] + (1,)))).astype(BF))
    return {"x": f(N, 128, 4 * NC), "u": f(N, 128, G * 512), "v": f(N, 128, G * 512), "w2": f(N, 128, 512)}
def setup_inputs_blocks(rng):
    d = setup_inputs(rng)
    for k in ("x", "u", "v", "w2"): d[k] = mx_ref.spread(d[k], rng, 4)
    return d
def setup_inputs_wide(rng):
    d = setup_inputs(rng)
    for k in ("x", "u", "v", "w2"): d[k] = mx_ref.flush((d[k].astype(np.float32) * np.exp2(rng.integers(-5, 6, (N, 1, 1))).astype(np.float32)).astype(BF))
    return d
def setup_inputs_zeros(rng):
    d = setup_inputs(rng); v = d["x"].reshape(N, 128, -1, 4).copy()
    v[np.broadcast_to((rng.random((N, 1, v.shape[2], 1)) < 0.33), v.shape)] = 0
    d["x"] = v.reshape(d["x"].shape)
    return d
def reference(x, u, v, w2):
    h = np.zeros((N, 128, 4 * NC), BF)
    for j in range(N):
        X = [mx_ref.quantize(x[j])]
        h[j] = tile(gate(layer(u[j], X), layer(v[j], X)))
    H = [mx_ref.quantize(h[j]) for j in range(N)]
    y = np.zeros((N, 128, N * NC), np.float32)
    for r in range(N):
        qw = mx_ref.quantize(w2[r])
        for j in range(N):
            y[r][:, NC * j:NC * j + NC] = mx_ref.matmul(qw, H[j])
    return {"y": y}

from concourse.bass import DstId, RemoteDMATransfer
from concourse.mybir import dt, AluOpType, ActivationFunctionType

N = 4
NC = 128
C = 0.00048828125
WORLD = 512
ENGINES = 16

SCRATCH = {
    "xin": ("sbuf", [128, 512], "bfloat16"),
    "uin": ("sbuf", [128, 1024], "bfloat16"),
    "vin": ("sbuf", [128, 1024], "bfloat16"),
    "win": ("sbuf", [128, 512], "bfloat16"),
    "xq": ("sbuf", [128, 128], "float8_e4m3fn_x4"), "xs": ("sbuf", [128, 128], "uint8"),
    "uq": ("sbuf", [128, 256], "float8_e4m3fn_x4"), "us": ("sbuf", [128, 256], "uint8"),
    "vq": ("sbuf", [128, 256], "float8_e4m3fn_x4"), "vs": ("sbuf", [128, 256], "uint8"),
    "wq": ("sbuf", [128, 128], "float8_e4m3fn_x4"), "ws": ("sbuf", [128, 128], "uint8"),
    "pu0": ("psum", [128, 512], "float32"), "pu1": ("psum", [128, 512], "float32"),
    "pv0": ("psum", [128, 512], "float32"), "pv1": ("psum", [128, 512], "float32"),
    "py0": ("psum", [128, 512], "float32"), "py1": ("psum", [128, 512], "float32"),
    "py2": ("psum", [128, 512], "float32"), "py3": ("psum", [128, 512], "float32"),
    "rl": ("sbuf", [128, 512], "float32"),
    "h": ("sbuf", [128, 512], "bfloat16"),
    "hq": ("sbuf", [128, N * NC], "float8_e4m3fn_x4"),
    "hs": ("sbuf", [128, N * NC], "uint8"),
    "yb": ("sbuf", [128, N * NC], "float32"),
}
SEMAPHORES = (["ldx", "ldu", "ldv", "ldw", "qx", "qu", "qv0", "qv1", "qh", "qw", "mu0", "mu1", "mv0", "mv1", "hd",
               "rs", "rc", "snt", "sts", "sta"]
              + ["r%d" % b for b in range(4)]
              + ["a%d" % j for j in range(N)] + ["my%d" % j for j in range(N)] + ["cp%d" % j for j in range(N)])


def _bits(m):
    return [e for e in range(ENGINES) if (m >> e) & 1]


def _mask(es):
    return sum(1 << e for e in es)


def _relays(cores, topo):
    used, via = set(cores), {}
    for s in cores:
        for d in cores:
            if s == d or topo.may_write(s, d):
                continue
            switch_first = topo.die(s) != topo.die(d)
            for c in range(WORLD):
                if c in used or topo.chip(c) != topo.chip(s) or topo.chip(c) != topo.chip(d):
                    continue
                if topo.die(c) != topo.die(d) or not (topo.may_write(s, c) and topo.may_write(c, d)):
                    continue
                if topo.same_plane(s, c) != switch_first:
                    continue
                via[(s, d)] = c
                used.add(c)
                break
    return via


def _codes(T, j):
    return T.hq[:, NC * j:NC * j + NC].bitcast(dt.uint8)


def _plane(T, j):
    return T.hs[:, NC * j:NC * j + NC]


def _relay_program(g, core, T, topo, s, d):
    j = T.rank_of(s)
    rid, pid = topo.addr(d, core)
    m = topo.mask(core, d)
    n_in = len(_bits(topo.mask(s, core))) // 2
    n_out = len(_bits(m))
    g.wait_ge(T.sem.rs, n_in)
    g.remote_dma(_plane(T, j), _plane(T, j), T.sem["a%d" % j], T.sem.snt, pid, rid, m)
    g.wait_ge(T.sem.rc, n_in)
    g.remote_dma(_codes(T, j), _codes(T, j), T.sem["a%d" % j], T.sem.snt, pid, rid, m)
    g.wait_ge(T.sem.snt, 2 * n_out)


def rank_program(g, core, T, topo):
    cores = list(T.cores)
    via = _relays(cores, topo)
    rank = T.rank_of(core)
    if rank is None:
        for (s, d), c in via.items():
            if c == core:
                _relay_program(g, core, T, topo, s, d)
        return

    sem = T.sem
    relu, copy = ActivationFunctionType.Relu, ActivationFunctionType.Copy
    near = [d for d in cores if d != core and topo.may_write(core, d)]
    far = [d for d in cores if d != core and not topo.may_write(core, d)]
    far.sort(key=lambda d: topo.same_plane(core, via[(core, d)]))

    g.sync.dma_start(T.xin[:], T.x[:]).then_inc(sem.ldx, 16)
    g.scalar.dma_start(T.uin[:], T.u[:]).then_inc(sem.ldu, 16)
    g.sync.dma_start(T.vin[:], T.v[:]).then_inc(sem.ldv, 16)
    g.sync.dma_start(T.win[:], T.w2[:]).then_inc(sem.ldw, 16)

    v = g.vector
    v.wait_ge(sem.ldx, 16)
    v.quantize_mx(T.xq[:], T.xs[:], T.xin[:]).then_inc(sem.qx, 1)
    v.wait_ge(sem.ldu, 16)
    v.quantize_mx(T.uq[:], T.us[:], T.uin[:]).then_inc(sem.qu, 1)
    v.wait_ge(sem.ldv, 16)
    v.quantize_mx(T.vq[:, 0:128], T.vs[:, 0:128], T.vin[:, 0:512]).then_inc(sem.qv0, 1)
    v.quantize_mx(T.vq[:, 128:256], T.vs[:, 128:256], T.vin[:, 512:1024]).then_inc(sem.qv1, 1)

    t = g.tensor
    t.wait_ge(sem.qx, 1)
    t.wait_ge(sem.qu, 1)
    t.matmul_mx(T.pu0[:, 0:NC], T.uq[:, 0:128], T.us[:, 0:128], T.xq[:], T.xs[:], True, True).then_inc(sem.mu0, 1)
    t.matmul_mx(T.pu1[:, 0:NC], T.uq[:, 128:256], T.us[:, 128:256], T.xq[:], T.xs[:], True, True).then_inc(sem.mu1, 1)
    t.wait_ge(sem.qv0, 1)
    t.matmul_mx(T.pv0[:, 0:NC], T.vq[:, 0:128], T.vs[:, 0:128], T.xq[:], T.xs[:], True, True).then_inc(sem.mv0, 1)
    t.wait_ge(sem.qv1, 1)
    t.matmul_mx(T.pv1[:, 0:NC], T.vq[:, 128:256], T.vs[:, 128:256], T.xq[:], T.xs[:], True, True).then_inc(sem.mv1, 1)

    a = g.scalar
    for i, (pu, mu) in enumerate(((T.pu0, sem.mu0), (T.pu1, sem.mu1))):
        a.wait_ge(mu, 1)
        for k, sc in enumerate((C, -C)):
            b = 2 * i + k
            a.activation(T.rl[:, NC * b:NC * b + NC], pu[:, 0:NC], relu, scale=sc).then_inc(sem["r%d" % b], 1)

    for i, (pv, mv) in enumerate(((T.pv0, sem.mv0), (T.pv1, sem.mv1))):
        v.wait_ge(mv, 1)
        for k in range(2):
            b = 2 * i + k
            v.wait_ge(sem["r%d" % b], 1)
            v.tensor_tensor(T.h[:, b:4 * NC:4], T.rl[:, NC * b:NC * b + NC], pv[:, 0:NC], AluOpType.mult).then_inc(sem.hd, 1)
    v.wait_ge(sem.hd, 4)
    v.quantize_mx(T.hq[:, NC * rank:NC * rank + NC], _plane(T, rank), T.h[:]).then_inc(sem.qh, 1)
    v.wait_ge(sem.ldw, 16)
    v.quantize_mx(T.wq[:], T.ws[:], T.win[:]).then_inc(sem.qw, 1)

    off = _bits(topo.mask(core, via[(core, far[0])]))
    sent = 0
    g.wait_ge(sem.qh, 1)
    for piece, rsem in ((_plane, sem.rs), (_codes, sem.rc)):
        trs = []
        for k, d in enumerate(far):
            c = via[(core, d)]
            rid, pid = topo.addr(c, core)
            es = off[1 - k::2]
            trs.append(RemoteDMATransfer(dst_ids=[DstId(rid=rid, pnc=pid)], dma_engine_mask=_mask(es), remote_sem=rsem,
                                         src=piece(T, rank), dst=piece(T, rank)))
            sent += len(es)
        g.remote_dma_fused(trs, local_sem=sem.snt)
    for d in near:
        rid, pid = topo.addr(d, core)
        es = [e for e in _bits(topo.mask(core, d)) if e not in off]
        for piece in (_plane, _codes):
            g.remote_dma(piece(T, rank), piece(T, rank), sem["a%d" % rank], sem.snt, pid, rid, _mask(es))
            sent += len(es)
    g.wait_ge(sem.snt, sent)

    order = [core] + near + far
    py = (T.py0, T.py1, T.py2, T.py3)
    for k, s in enumerate(order):
        j = T.rank_of(s)
        blk = slice(NC * j, NC * j + NC)
        if s == core:
            t.wait_ge(sem.qh, 1)
            t.wait_ge(sem.qw, 1)
        elif s in near:
            t.wait_ge(sem["a%d" % j], 2 * len([e for e in _bits(topo.mask(s, core)) if e not in off]))
        else:
            t.wait_ge(sem["a%d" % j], 2 * len(_bits(topo.mask(via[(s, core)], core))))
        t.matmul_mx(py[j][:, 0:NC], T.wq[:], T.ws[:], T.hq[:, blk], T.hs[:, blk], True, True).then_inc(sem["my%d" % j], 1)
        if k % 2 == 0:
            a.wait_ge(sem["my%d" % j], 1)
            a.activation(T.yb[:, blk], py[j][:, 0:NC], copy).then_inc(sem["cp%d" % j], 1)
            a.wait_ge(sem["cp%d" % j], 1)
            a.dma_start(T.y[:, blk], T.yb[:, blk]).then_inc(sem.sta, 16)
        else:
            v.wait_ge(sem["my%d" % j], 1)
            v.tensor_copy(T.yb[:, blk], py[j][:, 0:NC]).then_inc(sem["cp%d" % j], 1)
            g.sync.wait_ge(sem["cp%d" % j], 1)
            g.sync.dma_start(T.y[:, blk], T.yb[:, blk]).then_inc(sem.sts, 16)
    a.wait_ge(sem.sta, 32)
    g.sync.wait_ge(sem.sts, 32)
